import numpy as np
import ml_dtypes


def mxq(x, axis, fmt="e4m3"):
    dtype, down = {"e4m3": (ml_dtypes.float8_e4m3fn, 7), "e5m2": (ml_dtypes.float8_e5m2, 14)}[fmt]
    v = np.moveaxis(np.asarray(x, np.float32).astype(ml_dtypes.bfloat16).astype(np.float64), axis, -1)
    blocks = v.reshape(v.shape[:-1] + (-1, 32))
    amax = np.abs(blocks).max(-1, keepdims=True)
    byte = np.maximum(np.where(amax > 0, np.frexp(amax)[1] - 1 + 127, 0) - down, 1)
    scale = np.exp2(byte - 127.0)
    codes = (blocks / scale).astype(np.float32).astype(dtype).astype(np.float64)
    return np.moveaxis((codes * scale).reshape(v.shape), -1, axis)


WIDE = False


def mx_kscale(k):
    if not WIDE:
        return np.ones(k)
    levels = np.array([10, -10, 5, -5, 0])
    if k % 512:
        return np.exp2(np.random.permutation(np.resize(levels, k // 32))).repeat(32)
    a = np.empty((k // 512, 16))
    for p in range(k // 512):
        a[p, :8] = np.random.permutation(np.resize(levels, 8))
        for g in range(8):
            far = levels[np.abs(levels - a[p, g]) >= 10]
            a[p, g + 8] = far[np.random.randint(len(far))]
    return np.exp2(a.ravel()).repeat(32)


def f64(x):
    return np.asarray(x).astype(np.float64)


def striped(idx):
    return np.tile(idx.reshape(-1, 16).T, (8, 1)).astype(np.uint16)


def unstriped(offs):
    return offs[:16].T.reshape(-1).astype(np.int64)


def pack_weight(w):
    k, n = w.shape
    w = f64(np.asarray(w, np.float32).astype(ml_dtypes.bfloat16)).reshape(k // 32, 32, n)
    amax = np.abs(w).max(1)
    byte = np.clip(np.where(amax > 0, np.frexp(amax)[1] - 1 + 127 - 7, 1), 1, 254)
    scaled = (w * np.exp2(127.0 - byte)[:, None, :]).reshape(k, n).astype(np.float32)
    words = np.ascontiguousarray(scaled.reshape(k // 512, 128, 4, n).transpose(0, 1, 3, 2)).astype(ml_dtypes.float8_e4m3fn).view(np.uint8)
    return words, np.ascontiguousarray(byte.astype(np.uint8).reshape(k // 512, 16, n))


def unpack_weight(words, scales):
    g, p, n, _ = words.shape
    vals = np.ascontiguousarray(words).view(ml_dtypes.float8_e4m3fn).astype(np.float64) * np.repeat(np.exp2(scales.astype(np.float64) - 127.0), 8, axis=1)[..., None]
    return vals.transpose(0, 1, 3, 2).reshape(g * 512, n)


K, T, S, D, N, H, V, U = 512, 4096, 1024, 2, 256, 512, 512, 512


def setup_inputs():
    n = np.random.standard_normal
    s = mx_kscale(K)[:, None]
    u = mx_kscale(H)
    packed_xT = pack_weight(n((K, T)) * s)
    return {
        "x_words": packed_xT[0],
        "x_scales": packed_xT[1],
        "w1": (n((K, H)) / np.sqrt(K) / s).astype(np.float32),
        "sg": (np.where(np.random.uniform(size=(H, S)) < 0.5, -1.0, 1.0) * np.random.uniform(0.7, 1.3, (H, S))).astype(np.float32),
        "unit": (np.random.uniform(0.6, 1.4, (H, 1)) * u[:, None]).astype(np.float32),
        "w2": (n((H, N)) / np.sqrt(H) / u[:, None]).astype(np.float32),
        "offs": striped(np.random.permutation(T)[:S]),
        "ra": striped(np.random.randint(0, V, U)),
        "rb": striped(np.random.randint(0, V, U)),
    }


def reference(x_words, x_scales, w1, sg, unit, w2, offs, ra, rb):
    xq = unpack_weight(x_words, x_scales)[:, unstriped(offs)]
    y = mxq(f64(w1), 0, "e4m3").T @ xq
    hsum = y.reshape(len(y), -1, D).sum(axis=2)
    ea = hsum[:, unstriped(ra)]
    ys_ = y * f64(sg)
    hdif = ys_.reshape(len(ys_), -1, D).sum(axis=2)
    eb = hdif[:, unstriped(rb)]
    rot1 = ea + eb
    rot2 = hsum[:, unstriped(rb)] - hdif[:, unstriped(ra)]
    absm = np.maximum(np.abs(rot1), np.abs(rot2))
    hid = f64(unit) * (rot1 / (absm + 0.5) + 0.4 * rot2)
    return mxq(f64(w2), 0, "e4m3").T @ mxq(hid, 0, "e4m3")

@@ -1,0 +1,245 @@
+from contextlib import ExitStack
+
+import concourse.mybir as mybir
+
+K, T, S, H, V, N = 512, 4096, 1024, 512, 512, 256
+FLOPS = 2 * K * H * S + 2 * H * N * V
+
+F32 = mybir.dt.float32
+BF16 = mybir.dt.bfloat16
+I32 = mybir.dt.int32
+U32 = mybir.dt.uint32
+U16 = mybir.dt.uint16
+U8 = mybir.dt.uint8
+FP8X4 = mybir.dt.float8_e4m3fn_x4
+ALU = mybir.AluOpType
+ACT = mybir.ActivationFunctionType
+
+P = 128
+PACK = 4
+BANK = 512
+UNITS = ((0, 0, 512), (1, 0, 512), (2, 0, 512), (3, 0, 256), (3, 256, 128), (3, 384, 128))
+CHUNKS = ((0, 256), (256, 128), (384, 128))
+LEAD = (0, 0, 1, 1, 2, 2)
+WINDOW_LEAD = 2
+ON_GPSIMD = ()
+THREE_ON_SCALAR = ()
+SUMS_FIRST = (1, 2, 3)
+
+
+def tile_picked_yrotqv_norm_p_kernel(tc, x_words, x_scales, w1, sg, unit, w2, offs, ra, rb, out):
+    nc = tc.nc
+    with ExitStack() as ctx:
+        keep = ctx.enter_context(tc.tile_pool(name="keep", bufs=1))
+        ypsum = ctx.enter_context(tc.psum_pool(name="ypsum", bufs=6))
+        opsum = ctx.enter_context(tc.psum_pool(name="opsum", bufs=2))
+
+        offs_t = keep.tile([P, S // 16], U16, name="offs_t")
+        ra_t = keep.tile([P, V // 16], U16, name="ra_t")
+        rb_t = keep.tile([P, V // 16], U16, name="rb_t")
+        table_words = keep.tile([P, T], I32, name="table_words", align_bytes=64)
+        table_scales = keep.tile([P, T], U8, name="table_scales", align_bytes=64)
+        w1_raw = [keep.tile([P, PACK, H // 2], F32, name=f"w1_raw{h}") for h in range(2)]
+        sg_t = [keep.tile([P, S], F32, name=f"sg{t}") for t in range(PACK)]
+        unit_t = keep.tile([P, PACK], F32, name="unit_t")
+        w2_raw = keep.tile([P, PACK, N], F32, name="w2_raw")
+
+        nc.sync.dma_start(offs_t[:], offs)
+        nc.sync.dma_start(table_words[:], x_words[0].rearrange("p n t -> p (n t)").bitcast(I32))
+        nc.vector.memset(table_scales[:].bitcast(I32), 0)
+        for q in range(4):
+            nc.scalar.dma_start(table_scales[32 * q : 32 * q + 4, :].bitcast(I32), x_scales[0, 4 * q : 4 * q + 4, :].bitcast(I32))
+        w1_rows = w1.rearrange("(p j) c -> p j c", j=PACK)
+        for h in range(2):
+            nc.sync.dma_start(w1_raw[h][:], w1_rows[:, :, h * (H // 2) : (h + 1) * (H // 2)])
+        nc.sync.dma_start(unit_t[:], unit.rearrange("(p t) o -> p (t o)", t=PACK))
+        sg_rows = sg.rearrange("(p t) s -> p t s", t=PACK)
+        nc.sync.dma_start(sg_t[0][:], sg_rows[:, 0, :])
+        nc.sync.dma_start(ra_t[:], ra)
+        nc.sync.dma_start(rb_t[:], rb)
+        nc.sync.dma_start(w2_raw[:], w2.rearrange("(p j) c -> p j c", j=PACK))
+        for t in range(1, PACK):
+            nc.sync.dma_start(sg_t[t][:], sg_rows[:, t, :])
+
+        x_codes = []
+        x_bytes = []
+        for b in range(2):
+            picked = offs_t[:, b * (BANK // 16) : (b + 1) * (BANK // 16)]
+            gb = keep.tile([P, BANK], U8, name=f"x_bytes{b}", align_bytes=64)
+            nc.vector.tensor_copy(gb[:], table_scales[:].indirect(picked))
+            x_bytes.append(gb)
+        for b in range(2):
+            picked = offs_t[:, b * (BANK // 16) : (b + 1) * (BANK // 16)]
+            gw = keep.tile([P, BANK], U32, name=f"x_codes{b}", align_bytes=64)
+            nc.vector.tensor_copy(gw[:], table_words[:].bitcast(U32).indirect(picked))
+            x_codes.append(gw)
+
+        w1_grouped = keep.tile([P, PACK, P, PACK], BF16, name="w1_grouped", align_bytes=64)
+        for h, m0, m1, copy in ((0, 0, 64, nc.scalar.copy), (1, 0, 32, nc.vector.tensor_copy), (1, 32, 64, nc.scalar.copy)):
+            dst = w1_grouped[:, :, 64 * h + m0 : 64 * h + m1, :].rearrange("p t m j -> p m j t")
+            src = w1_raw[h][:, :, PACK * m0 : PACK * m1].rearrange("p j (m t) -> p m j t", t=PACK)
+            copy(dst, src)
+        w1_codes = []
+        w1_scales = []
+        for t in range(PACK):
+            wc = keep.tile([P, P], U32, name=f"w1_codes{t}", align_bytes=64)
+            ws = keep.tile([P, P], U8, name=f"w1_scales{t}", align_bytes=64)
+            nc.vector.quantize_mx(out=wc[:].bitcast(FP8X4), scales=ws[:], in_=w1_grouped[:, t, :, :].rearrange("p m j -> p (m j)"))
+            w1_codes.append(wc)
+            w1_scales.append(ws)
+
+        gain = keep.tile([P, PACK], F32, name="gain")
+        nc.vector.tensor_scalar(gain[:], unit_t[:], 0.4, None, ALU.mult)
+        size = keep.tile([P, PACK], F32, name="size")
+        nc.vector.scalar_tensor_tensor(size[:], unit_t[:], -1.0, unit_t[:], ALU.mult, ALU.max)
+        shift = keep.tile([P, PACK], F32, name="shift")
+        nc.vector.tensor_scalar(shift[:], size[:], 0.2, 2.0**-100, ALU.mult, ALU.max)
+
+        sum_win = [keep.tile([P, V + V], F32, name=f"sum_win{t}") for t in range(PACK)]
+        dif_win = [keep.tile([P, V + S], F32, name=f"dif_win{t}") for t in range(PACK)]
+
+        def windows(t):
+            scale = gain[:, t : t + 1]
+            banks = []
+            for b in range(2):
+                y = ypsum.tile([P, BANK], F32, name="y")
+                nc.tensor.matmul_mx(
+                    out=y[:],
+                    lhsT=w1_codes[t][:].bitcast(FP8X4),
+                    lhsT_scale=w1_scales[t][:],
+                    rhs=x_codes[b][:].bitcast(FP8X4),
+                    rhs_scale=x_bytes[b][:],
+                    start=True,
+                    stop=True,
+                )
+                banks.append(y)
+
+            def sums():
+                for b in range(2):
+                    c0 = b * (BANK // 2)
+                    nc.scalar.activation(sum_win[t][:, V + c0 : V + c0 + BANK // 2], banks[b][:, 1::2], ACT.Copy, scale=scale)
+                for b in range(2):
+                    c0 = b * (BANK // 2)
+                    nc.vector.scalar_tensor_tensor(
+                        sum_win[t][:, c0 : c0 + BANK // 2], banks[b][:, 0::2], scale, sum_win[t][:, V + c0 : V + c0 + BANK // 2], ALU.mult, ALU.add
+                    )
+
+            def differences():
+                for b in range(2):
+                    c0 = b * BANK
+                    nc.vector.scalar_tensor_tensor(
+                        dif_win[t][:, V + c0 : V + c0 + BANK], banks[b][:], scale, sg_t[t][:, c0 : c0 + BANK], ALU.mult, ALU.mult
+                    )
+                engine = nc.gpsimd if t in ON_GPSIMD else nc.vector
+                engine.tensor_tensor(dif_win[t][:, 0:V], dif_win[t][:, V::2], dif_win[t][:, V + 1 :: 2], ALU.add)
+
+            if t in SUMS_FIRST:
+                sums()
+                differences()
+            else:
+                differences()
+                sums()
+
+        rot = keep.tile([P, PACK, 2, V], F32, name="rot")
+        first = keep.tile([P, PACK, V], F32, name="first")
+        state = {}
+
+        def stage(s, k):
+            t, v0, n = UNITS[k]
+            la = ra_t[:, v0 // 16 : (v0 + n) // 16]
+            lb = rb_t[:, v0 // 16 : (v0 + n) // 16]
+            cols = slice(v0, v0 + n)
+
+            def fresh(name, width):
+                state[(name, k)] = keep.tile([P, width], F32, name=f"{name}{k}")
+                return state[(name, k)]
+
+            if s == 0:
+                nc.scalar.activation(fresh("sum_a", n)[:], sum_win[t][:].indirect(la), ACT.Copy)
+                nc.scalar.activation(fresh("sum_b", n)[:], sum_win[t][:].indirect(lb), ACT.Copy)
+                if k in THREE_ON_SCALAR:
+                    nc.scalar.activation(fresh("dif_a", n)[:], dif_win[t][:].indirect(la), ACT.Copy)
+            if s == 1:
+                nc.vector.tensor_tensor(rot[:, t, 1, cols], dif_win[t][:].indirect(lb), state[("sum_a", k)][:], ALU.add)
+                if k in THREE_ON_SCALAR:
+                    nc.vector.tensor_tensor(rot[:, t, 0, cols], state[("dif_a", k)][:], state[("sum_b", k)][:], ALU.subtract)
+                else:
+                    nc.vector.tensor_tensor(rot[:, t, 0, cols], dif_win[t][:].indirect(la), state[("sum_b", k)][:], ALU.subtract)
+            if s == 2:
+                mag = fresh("mag", 2 * n)
+                if n == V:
+                    nc.scalar.activation(mag[:], rot[:, t, :, :].rearrange("p r v -> p (r v)"), ACT.Abs)
+                else:
+                    nc.scalar.activation(mag[:, n : 2 * n], rot[:, t, 1, cols], ACT.Abs)
+                    nc.scalar.activation(mag[:, 0:n], rot[:, t, 0, cols], ACT.Abs)
+            if s == 3:
+                mag = state[("mag", k)]
+                nc.vector.tensor_tensor(fresh("absm", n)[:], mag[:, 0:n], mag[:, n : 2 * n], ALU.max)
+            if s == 4:
+                nc.scalar.activation(fresh("root", n)[:], state[("absm", k)][:], ACT.Abs_reciprocal_sqrt, bias=shift[:, t : t + 1])
+                nc.scalar.activation(fresh("recip", n)[:], state[("root", k)][:], ACT.Square)
+            if s == 5:
+                nc.vector.scalar_tensor_tensor(first[:, t, cols], rot[:, t, 1, cols], size[:, t : t + 1], state[("recip", k)][:], ALU.mult, ALU.mult)
+
+        w2_grouped = keep.tile([P, N, PACK], BF16, name="w2_grouped", align_bytes=64)
+        w2_codes = keep.tile([P, N], U32, name="w2_codes", align_bytes=64)
+        w2_scales = keep.tile([P, N], U8, name="w2_scales", align_bytes=64)
+
+        def quantize_w2():
+            nc.scalar.copy(
+                w2_grouped[:].rearrange("p (c i) j -> p c j i", i=4),
+                w2_raw[:].rearrange("p j (c i) -> p c j i", i=4),
+            )
+            nc.vector.quantize_mx(out=w2_codes[:].bitcast(FP8X4), scales=w2_scales[:], in_=w2_grouped[:].rearrange("p c j -> p (c j)"))
+
+        out_rows = out.rearrange("(a p) v -> p a v", p=P)
+
+        def finish(v0, n):
+            grouped = keep.tile([P, n, PACK], BF16, name=f"hid_grouped{v0}", align_bytes=64)
+            nc.vector.tensor_tensor(
+                grouped[:].rearrange("p (c i) t -> p c t i", i=4),
+                first[:, :, v0 : v0 + n].rearrange("p t (c i) -> p c t i", i=4),
+                rot[:, :, 0, v0 : v0 + n].rearrange("p t (c i) -> p c t i", i=4),
+                ALU.subtract,
+            )
+            codes = keep.tile([P, n], U32, name=f"hid_codes{v0}", align_bytes=64)
+            scales = keep.tile([P, n], U8, name=f"hid_scales{v0}", align_bytes=64)
+            nc.vector.quantize_mx(out=codes[:].bitcast(FP8X4), scales=scales[:], in_=grouped[:].rearrange("p c t -> p (c t)"))
+            acc = opsum.tile([P, 2, n], F32, name="acc")
+            for a in range(2):
+                nc.tensor.matmul_mx(
+                    out=acc[:, a, :],
+                    lhsT=w2_codes[:, a * P : (a + 1) * P].bitcast(FP8X4),
+                    lhsT_scale=w2_scales[:, a * P : (a + 1) * P],
+                    rhs=codes[:].bitcast(FP8X4),
+                    rhs_scale=scales[:],
+                    start=True,
+                    stop=True,
+                )
+            result = keep.tile([P, 2, n], F32, name=f"result{v0}")
+            nc.scalar.copy(result[:], acc[:])
+            nc.sync.dma_start(out_rows[:, :, v0 : v0 + n], result[:])
+
+        first_unit = {}
+        for k, (t, v0, n) in enumerate(UNITS):
+            first_unit.setdefault(t, k)
+        ended = set()
+        finished = 0
+        for step in range(-WINDOW_LEAD, len(UNITS) + max(LEAD)):
+            for t in range(PACK):
+                if first_unit[t] - WINDOW_LEAD == step:
+                    windows(t)
+                    if t == 0:
+                        quantize_w2()
+            for s in range(6):
+                k = step - LEAD[s]
+                if 0 <= k < len(UNITS):
+                    stage(s, k)
+                    if s == 5:
+                        ended.add(k)
+                        while finished < len(CHUNKS):
+                            c0, cn = CHUNKS[finished]
+                            if not all(i in ended for i, (t, a, b) in enumerate(UNITS) if a < c0 + cn and a + b > c0):
+                                break
+                            finish(c0, cn)
+                            finished = finished + 1

@@ -38,13 +38,14 @@ def tile_picked_yrotqv_norm_p_kernel(tc, x_words, x_scales, w1, sg, unit, w2, of
         ra_t = keep.tile([P, V // 16], U16, name="ra_t")
         rb_t = keep.tile([P, V // 16], U16, name="rb_t")
         table_words = keep.tile([P, T], I32, name="table_words", align_bytes=64)
-        table_scales = keep.tile([P, T], U8, name="table_scales", align_bytes=64)
+        table_scales = keep.tile([P, T], U8, name="table_scales", tag="table_then_codes", align_bytes=64)
         w1_raw = [keep.tile([P, PACK, H // 2], F32, name=f"w1_raw{h}") for h in range(2)]
         sg_t = [keep.tile([P, S], F32, name=f"sg{t}") for t in range(PACK)]
         unit_t = keep.tile([P, PACK], F32, name="unit_t")
         w2_raw = keep.tile([P, PACK, N], F32, name="w2_raw")
 
         nc.sync.dma_start(offs_t[:], offs)
+        nc.sync.dma_start(unit_t[:], unit.rearrange("(p t) o -> p (t o)", t=PACK))
         nc.sync.dma_start(table_words[:], x_words[0].rearrange("p n t -> p (n t)").bitcast(I32))
         nc.vector.memset(table_scales[:].bitcast(I32), 0)
         for q in range(4):
@@ -52,7 +53,6 @@ def tile_picked_yrotqv_norm_p_kernel(tc, x_words, x_scales, w1, sg, unit, w2, of
         w1_rows = w1.rearrange("(p j) c -> p j c", j=PACK)
         for h in range(2):
             nc.sync.dma_start(w1_raw[h][:], w1_rows[:, :, h * (H // 2) : (h + 1) * (H // 2)])
-        nc.sync.dma_start(unit_t[:], unit.rearrange("(p t) o -> p (t o)", t=PACK))
         sg_rows = sg.rearrange("(p t) s -> p t s", t=PACK)
         nc.sync.dma_start(sg_t[0][:], sg_rows[:, 0, :])
         nc.sync.dma_start(ra_t[:], ra)
@@ -61,6 +61,8 @@ def tile_picked_yrotqv_norm_p_kernel(tc, x_words, x_scales, w1, sg, unit, w2, of
         for t in range(1, PACK):
             nc.sync.dma_start(sg_t[t][:], sg_rows[:, t, :])
 
+        warm_out = keep.tile([P, 1], F32, name="warm_out")
+        nc.scalar.activation(warm_out[:], unit_t[:, 0:1], ACT.Abs_reciprocal_sqrt)
         x_codes = []
         x_bytes = []
         for b in range(2):
@@ -68,16 +70,17 @@ def tile_picked_yrotqv_norm_p_kernel(tc, x_words, x_scales, w1, sg, unit, w2, of
             gb = keep.tile([P, BANK], U8, name=f"x_bytes{b}", align_bytes=64)
             nc.vector.tensor_copy(gb[:], table_scales[:].indirect(picked))
             x_bytes.append(gb)
+        picked_words = keep.tile([P, S], U32, name="picked_words", tag="table_then_codes", align_bytes=64)
         for b in range(2):
             picked = offs_t[:, b * (BANK // 16) : (b + 1) * (BANK // 16)]
-            gw = keep.tile([P, BANK], U32, name=f"x_codes{b}", align_bytes=64)
-            nc.vector.tensor_copy(gw[:], table_words[:].bitcast(U32).indirect(picked))
+            gw = picked_words[:, b * BANK : (b + 1) * BANK]
+            nc.vector.tensor_copy(gw, table_words[:].bitcast(U32).indirect(picked))
             x_codes.append(gw)
 
         w1_grouped = keep.tile([P, PACK, P, PACK], BF16, name="w1_grouped", align_bytes=64)
         for h, m0, m1, copy in ((0, 0, 64, nc.scalar.copy), (1, 0, 32, nc.vector.tensor_copy), (1, 32, 64, nc.scalar.copy)):
-            dst = w1_grouped[:, :, 64 * h + m0 : 64 * h + m1, :].rearrange("p t m j -> p m j t")
-            src = w1_raw[h][:, :, PACK * m0 : PACK * m1].rearrange("p j (m t) -> p m j t", t=PACK)
+            dst = w1_grouped[:, :, 64 * h + m0 : 64 * h + m1, :].rearrange("p t m j -> p m t j")
+            src = w1_raw[h][:, :, PACK * m0 : PACK * m1].rearrange("p j (m t) -> p m t j", t=PACK)
             copy(dst, src)
         w1_codes = []
         w1_scales = []
@@ -107,7 +110,7 @@ def tile_picked_yrotqv_norm_p_kernel(tc, x_words, x_scales, w1, sg, unit, w2, of
                     out=y[:],
                     lhsT=w1_codes[t][:].bitcast(FP8X4),
                     lhsT_scale=w1_scales[t][:],
-                    rhs=x_codes[b][:].bitcast(FP8X4),
+                    rhs=x_codes[b].bitcast(FP8X4),
                     rhs_scale=x_bytes[b][:],
                     start=True,
                     stop=True,
@@ -187,8 +190,8 @@ def tile_picked_yrotqv_norm_p_kernel(tc, x_words, x_scales, w1, sg, unit, w2, of
 
         def quantize_w2():
             nc.scalar.copy(
-                w2_grouped[:].rearrange("p (c i) j -> p c j i", i=4),
-                w2_raw[:].rearrange("p j (c i) -> p c j i", i=4),
+                w2_grouped[:].rearrange("p (c i) j -> p c j i", i=2),
+                w2_raw[:].rearrange("p j (c i) -> p c j i", i=2),
             )
             nc.vector.quantize_mx(out=w2_codes[:].bitcast(FP8X4), scales=w2_scales[:], in_=w2_grouped[:].rearrange("p c j -> p (c j)"))
 
@@ -197,9 +200,9 @@ def tile_picked_yrotqv_norm_p_kernel(tc, x_words, x_scales, w1, sg, unit, w2, of
         def finish(v0, n):
             grouped = keep.tile([P, n, PACK], BF16, name=f"hid_grouped{v0}", align_bytes=64)
             nc.vector.tensor_tensor(
-                grouped[:].rearrange("p (c i) t -> p c t i", i=4),
-                first[:, :, v0 : v0 + n].rearrange("p t (c i) -> p c t i", i=4),
-                rot[:, :, 0, v0 : v0 + n].rearrange("p t (c i) -> p c t i", i=4),
+                grouped[:].rearrange("p (c i) t -> p c t i", i=2),
+                first[:, :, v0 : v0 + n].rearrange("p t (c i) -> p c t i", i=2),
+                rot[:, :, 0, v0 : v0 + n].rearrange("p t (c i) -> p c t i", i=2),
                 ALU.subtract,
             )
             codes = keep.tile([P, n], U32, name=f"hid_codes{v0}", align_bytes=64)

@@ -18,13 +18,14 @@ ACT = mybir.ActivationFunctionType
 P = 128
 PACK = 4
 BANK = 512
-UNITS = ((0, 0, 512), (1, 0, 512), (2, 0, 512), (3, 0, 256), (3, 256, 128), (3, 384, 128))
-CHUNKS = ((0, 256), (256, 128), (384, 128))
-LEAD = (0, 0, 1, 1, 2, 2)
+PAIRS = BANK // 2
+LIST_ROWS = 16
+MX_ALIGN = 64
+TINY = 2.0**-100
+
+PIECES = ((0, 256), (256, 128), (384, 128))
+TASKS = tuple((t, 0, V) for t in range(PACK - 1)) + tuple((PACK - 1, v0, n) for v0, n in PIECES)
 WINDOW_LEAD = 2
-ON_GPSIMD = ()
-THREE_ON_SCALAR = ()
-SUMS_FIRST = (1, 2, 3)
 
 
 def tile_picked_yrotqv_norm_p_kernel(tc, x_words, x_scales, w1, sg, unit, w2, offs, ra, rb, out):
@@ -34,69 +35,64 @@ def tile_picked_yrotqv_norm_p_kernel(tc, x_words, x_scales, w1, sg, unit, w2, of
         ypsum = ctx.enter_context(tc.psum_pool(name="ypsum", bufs=6))
         opsum = ctx.enter_context(tc.psum_pool(name="opsum", bufs=2))
 
-        offs_t = keep.tile([P, S // 16], U16, name="offs_t")
-        ra_t = keep.tile([P, V // 16], U16, name="ra_t")
-        rb_t = keep.tile([P, V // 16], U16, name="rb_t")
-        table_words = keep.tile([P, T], I32, name="table_words", align_bytes=64)
-        table_scales = keep.tile([P, T], U8, name="table_scales", tag="table_then_codes", align_bytes=64)
-        w1_raw = [keep.tile([P, PACK, H // 2], F32, name=f"w1_raw{h}") for h in range(2)]
-        sg_t = [keep.tile([P, S], F32, name=f"sg{t}") for t in range(PACK)]
-        unit_t = keep.tile([P, PACK], F32, name="unit_t")
-        w2_raw = keep.tile([P, PACK, N], F32, name="w2_raw")
+        offs_t = keep.tile([P, S // LIST_ROWS], U16, name="offs_t")
+        ra_t = keep.tile([P, V // LIST_ROWS], U16, name="ra_t")
+        rb_t = keep.tile([P, V // LIST_ROWS], U16, name="rb_t")
+        unit_t = keep.tile([P, PACK], F32, name="unit_t", tag="unit_then_words", align_bytes=MX_ALIGN)
+        table_scales = keep.tile([P, T], U8, name="table_scales", tag="scales_then_inputs", align_bytes=MX_ALIGN)
+        w1_raw = keep.tile([P, PACK, H], F32, name="w1_raw")
 
+        nc.scalar.dma_start(unit_t[:], unit.rearrange("(p t) o -> p (t o)", t=PACK))
         nc.sync.dma_start(offs_t[:], offs)
-        nc.sync.dma_start(unit_t[:], unit.rearrange("(p t) o -> p (t o)", t=PACK))
-        nc.sync.dma_start(table_words[:], x_words[0].rearrange("p n t -> p (n t)").bitcast(I32))
+        nc.sync.dma_start(w1_raw[:], w1.rearrange("(p j) c -> p j c", j=PACK))
+        nc.sync.dma_start(ra_t[:], ra)
+        nc.sync.dma_start(rb_t[:], rb)
         nc.vector.memset(table_scales[:].bitcast(I32), 0)
         for q in range(4):
             nc.scalar.dma_start(table_scales[32 * q : 32 * q + 4, :].bitcast(I32), x_scales[0, 4 * q : 4 * q + 4, :].bitcast(I32))
-        w1_rows = w1.rearrange("(p j) c -> p j c", j=PACK)
-        for h in range(2):
-            nc.sync.dma_start(w1_raw[h][:], w1_rows[:, :, h * (H // 2) : (h + 1) * (H // 2)])
-        sg_rows = sg.rearrange("(p t) s -> p t s", t=PACK)
-        nc.sync.dma_start(sg_t[0][:], sg_rows[:, 0, :])
-        nc.sync.dma_start(ra_t[:], ra)
-        nc.sync.dma_start(rb_t[:], rb)
-        nc.sync.dma_start(w2_raw[:], w2.rearrange("(p j) c -> p j c", j=PACK))
-        for t in range(1, PACK):
-            nc.sync.dma_start(sg_t[t][:], sg_rows[:, t, :])
-
-        warm_out = keep.tile([P, 1], F32, name="warm_out")
-        nc.scalar.activation(warm_out[:], unit_t[:, 0:1], ACT.Abs_reciprocal_sqrt)
-        x_codes = []
-        x_bytes = []
-        for b in range(2):
-            picked = offs_t[:, b * (BANK // 16) : (b + 1) * (BANK // 16)]
-            gb = keep.tile([P, BANK], U8, name=f"x_bytes{b}", align_bytes=64)
-            nc.vector.tensor_copy(gb[:], table_scales[:].indirect(picked))
-            x_bytes.append(gb)
-        picked_words = keep.tile([P, S], U32, name="picked_words", tag="table_then_codes", align_bytes=64)
-        for b in range(2):
-            picked = offs_t[:, b * (BANK // 16) : (b + 1) * (BANK // 16)]
-            gw = picked_words[:, b * BANK : (b + 1) * BANK]
-            nc.vector.tensor_copy(gw, table_words[:].bitcast(U32).indirect(picked))
-            x_codes.append(gw)
-
-        w1_grouped = keep.tile([P, PACK, P, PACK], BF16, name="w1_grouped", align_bytes=64)
-        for h, m0, m1, copy in ((0, 0, 64, nc.scalar.copy), (1, 0, 32, nc.vector.tensor_copy), (1, 32, 64, nc.scalar.copy)):
-            dst = w1_grouped[:, :, 64 * h + m0 : 64 * h + m1, :].rearrange("p t m j -> p m t j")
-            src = w1_raw[h][:, :, PACK * m0 : PACK * m1].rearrange("p j (m t) -> p m t j", t=PACK)
-            copy(dst, src)
-        w1_codes = []
-        w1_scales = []
-        for t in range(PACK):
-            wc = keep.tile([P, P], U32, name=f"w1_codes{t}", align_bytes=64)
-            ws = keep.tile([P, P], U8, name=f"w1_scales{t}", align_bytes=64)
-            nc.vector.quantize_mx(out=wc[:].bitcast(FP8X4), scales=ws[:], in_=w1_grouped[:, t, :, :].rearrange("p m j -> p (m j)"))
-            w1_codes.append(wc)
-            w1_scales.append(ws)
 
         gain = keep.tile([P, PACK], F32, name="gain")
         nc.vector.tensor_scalar(gain[:], unit_t[:], 0.4, None, ALU.mult)
-        size = keep.tile([P, PACK], F32, name="size")
-        nc.vector.scalar_tensor_tensor(size[:], unit_t[:], -1.0, unit_t[:], ALU.mult, ALU.max)
+        warm_out = keep.tile([P, 1], F32, name="warm_out")
+        nc.scalar.activation(warm_out[:], gain[:, 0:1], ACT.Abs_reciprocal_sqrt)
+
+        table_words = keep.tile([P, T], I32, name="table_words", tag="unit_then_words", align_bytes=MX_ALIGN)
+        nc.sync.dma_start(table_words[:], x_words[0].rearrange("p n t -> p (n t)").bitcast(I32))
+
+        picked = [offs_t[:, b * (BANK // LIST_ROWS) : (b + 1) * (BANK // LIST_ROWS)] for b in range(2)]
+        x_bytes = []
+        for b in range(2):
+            gathered_bytes = keep.tile([P, BANK], U8, name=f"x_bytes{b}", align_bytes=MX_ALIGN)
+            nc.vector.tensor_copy(gathered_bytes[:], table_scales[:].indirect(picked[b]))
+            x_bytes.append(gathered_bytes)
+
+        inputs = keep.tile([P, (1 + PACK) * S], F32, name="inputs", tag="scales_then_inputs", align_bytes=MX_ALIGN)
+        w2_raw = inputs[:, 0 : PACK * N].rearrange("p (j c) -> p j c", j=PACK)
+        sg_t = [inputs[:, (1 + t) * S : (2 + t) * S] for t in range(PACK)]
+        sg_rows = sg.rearrange("(p t) s -> p t s", t=PACK)
+        nc.sync.dma_start(sg_t[0], sg_rows[:, 0, :])
+        nc.sync.dma_start(w2_raw, w2.rearrange("(p j) c -> p j c", j=PACK))
+        for t in range(1, PACK):
+            nc.sync.dma_start(sg_t[t], sg_rows[:, t, :])
+
+        x_codes = []
+        for b in range(2):
+            gathered_words = keep.tile([P, BANK], U32, name=f"x_codes{b}", tag=f"x_codes{b}", align_bytes=MX_ALIGN)
+            nc.vector.tensor_copy(gathered_words[:], table_words[:].bitcast(U32).indirect(picked[b]))
+            x_codes.append(gathered_words)
+
+        w1_grouped = keep.tile([P, PACK, P, PACK], BF16, name="w1_grouped", align_bytes=MX_ALIGN)
+        nc.scalar.copy(w1_grouped[:].rearrange("p t m j -> p m t j"), w1_raw[:].rearrange("p j (m t) -> p m t j", t=PACK))
+        w1_codes = keep.tile([P, H], U32, name="w1_codes", align_bytes=MX_ALIGN)
+        w1_scales = keep.tile([P, H], U8, name="w1_scales", align_bytes=MX_ALIGN)
+        nc.vector.quantize_mx(out=w1_codes[:].bitcast(FP8X4), scales=w1_scales[:], in_=w1_grouped[:].rearrange("p t m j -> p (t m j)"))
+
+        gain_size = keep.tile([P, PACK], F32, name="gain_size")
+        nc.vector.scalar_tensor_tensor(gain_size[:], gain[:], -1.0, gain[:], ALU.mult, ALU.max)
+        unit_size = keep.tile([P, PACK], F32, name="unit_size")
+        nc.vector.tensor_scalar(unit_size[:], gain_size[:], 2.5, None, ALU.mult)
         shift = keep.tile([P, PACK], F32, name="shift")
-        nc.vector.tensor_scalar(shift[:], size[:], 0.2, 2.0**-100, ALU.mult, ALU.max)
+        nc.vector.tensor_scalar(shift[:], gain_size[:], 0.5, TINY, ALU.mult, ALU.max)
 
         sum_win = [keep.tile([P, V + V], F32, name=f"sum_win{t}") for t in range(PACK)]
         dif_win = [keep.tile([P, V + S], F32, name=f"dif_win{t}") for t in range(PACK)]
@@ -108,141 +104,127 @@ def tile_picked_yrotqv_norm_p_kernel(tc, x_words, x_scales, w1, sg, unit, w2, of
                 y = ypsum.tile([P, BANK], F32, name="y")
                 nc.tensor.matmul_mx(
                     out=y[:],
-                    lhsT=w1_codes[t][:].bitcast(FP8X4),
-                    lhsT_scale=w1_scales[t][:],
-                    rhs=x_codes[b].bitcast(FP8X4),
+                    lhsT=w1_codes[:, t * P : (t + 1) * P].bitcast(FP8X4),
+                    lhsT_scale=w1_scales[:, t * P : (t + 1) * P],
+                    rhs=x_codes[b][:].bitcast(FP8X4),
                     rhs_scale=x_bytes[b][:],
                     start=True,
                     stop=True,
                 )
                 banks.append(y)
-
-            def sums():
-                for b in range(2):
-                    c0 = b * (BANK // 2)
-                    nc.scalar.activation(sum_win[t][:, V + c0 : V + c0 + BANK // 2], banks[b][:, 1::2], ACT.Copy, scale=scale)
-                for b in range(2):
-                    c0 = b * (BANK // 2)
-                    nc.vector.scalar_tensor_tensor(
-                        sum_win[t][:, c0 : c0 + BANK // 2], banks[b][:, 0::2], scale, sum_win[t][:, V + c0 : V + c0 + BANK // 2], ALU.mult, ALU.add
-                    )
-
-            def differences():
-                for b in range(2):
-                    c0 = b * BANK
-                    nc.vector.scalar_tensor_tensor(
-                        dif_win[t][:, V + c0 : V + c0 + BANK], banks[b][:], scale, sg_t[t][:, c0 : c0 + BANK], ALU.mult, ALU.mult
-                    )
-                engine = nc.gpsimd if t in ON_GPSIMD else nc.vector
-                engine.tensor_tensor(dif_win[t][:, 0:V], dif_win[t][:, V::2], dif_win[t][:, V + 1 :: 2], ALU.add)
-
-            if t in SUMS_FIRST:
-                sums()
-                differences()
-            else:
-                differences()
-                sums()
+            odd = [sum_win[t][:, V + b * PAIRS : V + (b + 1) * PAIRS] for b in range(2)]
+            for b in range(2):
+                nc.scalar.activation(odd[b], banks[b][:, 1::2], ACT.Copy, scale=scale)
+            for b in range(2):
+                nc.vector.scalar_tensor_tensor(sum_win[t][:, b * PAIRS : (b + 1) * PAIRS], banks[b][:, 0::2], scale, odd[b], ALU.mult, ALU.add)
+            for b in range(2):
+                nc.vector.scalar_tensor_tensor(
+                    dif_win[t][:, V + b * BANK : V + (b + 1) * BANK], banks[b][:], scale, sg_t[t][:, b * BANK : (b + 1) * BANK], ALU.mult, ALU.mult
+                )
+            adder = nc.gpsimd if t < PACK - 1 else nc.vector
+            adder.tensor_tensor(dif_win[t][:, 0:V], dif_win[t][:, V::2], dif_win[t][:, V + 1 :: 2], ALU.add)
 
         rot = keep.tile([P, PACK, 2, V], F32, name="rot")
         first = keep.tile([P, PACK, V], F32, name="first")
-        state = {}
+        held = {}
 
-        def stage(s, k):
-            t, v0, n = UNITS[k]
-            la = ra_t[:, v0 // 16 : (v0 + n) // 16]
-            lb = rb_t[:, v0 // 16 : (v0 + n) // 16]
-            cols = slice(v0, v0 + n)
+        def fresh(name, k, width):
+            held[(name, k)] = keep.tile([P, width], F32, name=f"{name}{k}")
+            return held[(name, k)]
 
-            def fresh(name, width):
-                state[(name, k)] = keep.tile([P, width], F32, name=f"{name}{k}")
-                return state[(name, k)]
+        def lists(k):
+            v0, n = TASKS[k][1:]
+            cols = slice(v0 // LIST_ROWS, (v0 + n) // LIST_ROWS)
+            return ra_t[:, cols], rb_t[:, cols]
 
-            if s == 0:
-                nc.scalar.activation(fresh("sum_a", n)[:], sum_win[t][:].indirect(la), ACT.Copy)
-                nc.scalar.activation(fresh("sum_b", n)[:], sum_win[t][:].indirect(lb), ACT.Copy)
-                if k in THREE_ON_SCALAR:
-                    nc.scalar.activation(fresh("dif_a", n)[:], dif_win[t][:].indirect(la), ACT.Copy)
-            if s == 1:
-                nc.vector.tensor_tensor(rot[:, t, 1, cols], dif_win[t][:].indirect(lb), state[("sum_a", k)][:], ALU.add)
-                if k in THREE_ON_SCALAR:
-                    nc.vector.tensor_tensor(rot[:, t, 0, cols], state[("dif_a", k)][:], state[("sum_b", k)][:], ALU.subtract)
-                else:
-                    nc.vector.tensor_tensor(rot[:, t, 0, cols], dif_win[t][:].indirect(la), state[("sum_b", k)][:], ALU.subtract)
-            if s == 2:
-                mag = fresh("mag", 2 * n)
-                if n == V:
-                    nc.scalar.activation(mag[:], rot[:, t, :, :].rearrange("p r v -> p (r v)"), ACT.Abs)
-                else:
-                    nc.scalar.activation(mag[:, n : 2 * n], rot[:, t, 1, cols], ACT.Abs)
-                    nc.scalar.activation(mag[:, 0:n], rot[:, t, 0, cols], ACT.Abs)
-            if s == 3:
-                mag = state[("mag", k)]
-                nc.vector.tensor_tensor(fresh("absm", n)[:], mag[:, 0:n], mag[:, n : 2 * n], ALU.max)
-            if s == 4:
-                nc.scalar.activation(fresh("root", n)[:], state[("absm", k)][:], ACT.Abs_reciprocal_sqrt, bias=shift[:, t : t + 1])
-                nc.scalar.activation(fresh("recip", n)[:], state[("root", k)][:], ACT.Square)
-            if s == 5:
-                nc.vector.scalar_tensor_tensor(first[:, t, cols], rot[:, t, 1, cols], size[:, t : t + 1], state[("recip", k)][:], ALU.mult, ALU.mult)
+        def gather_sums(k):
+            t, n = TASKS[k][0], TASKS[k][2]
+            by_ra, by_rb = lists(k)
+            nc.scalar.activation(fresh("sum_a", k, n)[:], sum_win[t][:].indirect(by_ra), ACT.Copy)
+            nc.scalar.activation(fresh("sum_b", k, n)[:], sum_win[t][:].indirect(by_rb), ACT.Copy)
 
-        w2_grouped = keep.tile([P, N, PACK], BF16, name="w2_grouped", align_bytes=64)
-        w2_codes = keep.tile([P, N], U32, name="w2_codes", align_bytes=64)
-        w2_scales = keep.tile([P, N], U8, name="w2_scales", align_bytes=64)
+        def rotate(k):
+            t, v0, n = TASKS[k]
+            by_ra, by_rb = lists(k)
+            nc.vector.tensor_tensor(rot[:, t, 1, v0 : v0 + n], dif_win[t][:].indirect(by_rb), held[("sum_a", k)][:], ALU.add)
+            nc.vector.tensor_tensor(rot[:, t, 0, v0 : v0 + n], dif_win[t][:].indirect(by_ra), held[("sum_b", k)][:], ALU.subtract)
+
+        def magnitudes(k):
+            t, v0, n = TASKS[k]
+            mag = fresh("mag", k, 2 * n)
+            if n == V:
+                nc.scalar.activation(mag[:], rot[:, t, :, :].rearrange("p r v -> p (r v)"), ACT.Abs)
+            else:
+                nc.scalar.activation(mag[:, n : 2 * n], rot[:, t, 1, v0 : v0 + n], ACT.Abs)
+                nc.scalar.activation(mag[:, 0:n], rot[:, t, 0, v0 : v0 + n], ACT.Abs)
+
+        def larger(k):
+            n = TASKS[k][2]
+            mag = held[("mag", k)]
+            nc.vector.tensor_tensor(fresh("absm", k, n)[:], mag[:, 0:n], mag[:, n : 2 * n], ALU.max)
+
+        def reciprocal(k):
+            t, n = TASKS[k][0], TASKS[k][2]
+            nc.scalar.activation(fresh("root", k, n)[:], held[("absm", k)][:], ACT.Abs_reciprocal_sqrt, bias=shift[:, t : t + 1])
+            nc.scalar.activation(fresh("recip", k, n)[:], held[("root", k)][:], ACT.Square)
+
+        def first_term(k):
+            t, v0, n = TASKS[k]
+            nc.vector.scalar_tensor_tensor(
+                first[:, t, v0 : v0 + n], rot[:, t, 1, v0 : v0 + n], unit_size[:, t : t + 1], held[("recip", k)][:], ALU.mult, ALU.mult
+            )
+
+        w2_grouped = keep.tile([P, N, PACK], BF16, name="w2_grouped", align_bytes=MX_ALIGN)
+        w2_scales = keep.tile([P, N], U8, name="w2_scales", align_bytes=MX_ALIGN)
+
+        def round_w2():
+            nc.gpsimd.tensor_scalar(w2_grouped[:], w2_raw.rearrange("p j c -> p c j"), 1.0, 0.0, ALU.mult, ALU.add)
 
         def quantize_w2():
-            nc.scalar.copy(
-                w2_grouped[:].rearrange("p (c i) j -> p c j i", i=2),
-                w2_raw[:].rearrange("p j (c i) -> p c j i", i=2),
-            )
-            nc.vector.quantize_mx(out=w2_codes[:].bitcast(FP8X4), scales=w2_scales[:], in_=w2_grouped[:].rearrange("p c j -> p (c j)"))
+            held["w2_codes"] = keep.tile([P, N], U32, name="w2_codes", tag="x_codes1", align_bytes=MX_ALIGN)
+            nc.vector.quantize_mx(out=held["w2_codes"][:].bitcast(FP8X4), scales=w2_scales[:], in_=w2_grouped[:].rearrange("p c j -> p (c j)"))
 
         out_rows = out.rearrange("(a p) v -> p a v", p=P)
 
         def finish(v0, n):
-            grouped = keep.tile([P, n, PACK], BF16, name=f"hid_grouped{v0}", align_bytes=64)
+            grouped = keep.tile([P, n, PACK], BF16, name=f"hid_grouped{v0}", align_bytes=MX_ALIGN)
             nc.vector.tensor_tensor(
                 grouped[:].rearrange("p (c i) t -> p c t i", i=2),
                 first[:, :, v0 : v0 + n].rearrange("p t (c i) -> p c t i", i=2),
                 rot[:, :, 0, v0 : v0 + n].rearrange("p t (c i) -> p c t i", i=2),
                 ALU.subtract,
             )
-            codes = keep.tile([P, n], U32, name=f"hid_codes{v0}", align_bytes=64)
-            scales = keep.tile([P, n], U8, name=f"hid_scales{v0}", align_bytes=64)
+            codes = keep.tile([P, n], U32, name=f"hid_codes{v0}", align_bytes=MX_ALIGN)
+            scales = keep.tile([P, n], U8, name=f"hid_scales{v0}", align_bytes=MX_ALIGN)
             nc.vector.quantize_mx(out=codes[:].bitcast(FP8X4), scales=scales[:], in_=grouped[:].rearrange("p c t -> p (c t)"))
-            acc = opsum.tile([P, 2, n], F32, name="acc")
-            for a in range(2):
+            acc = opsum.tile([P, N // P, n], F32, name="acc")
+            for a in range(N // P):
                 nc.tensor.matmul_mx(
                     out=acc[:, a, :],
-                    lhsT=w2_codes[:, a * P : (a + 1) * P].bitcast(FP8X4),
+                    lhsT=held["w2_codes"][:, a * P : (a + 1) * P].bitcast(FP8X4),
                     lhsT_scale=w2_scales[:, a * P : (a + 1) * P],
                     rhs=codes[:].bitcast(FP8X4),
                     rhs_scale=scales[:],
                     start=True,
                     stop=True,
                 )
-            result = keep.tile([P, 2, n], F32, name=f"result{v0}")
+            result = keep.tile([P, N // P, n], F32, name=f"result{v0}")
             nc.scalar.copy(result[:], acc[:])
             nc.sync.dma_start(out_rows[:, :, v0 : v0 + n], result[:])
 
-        first_unit = {}
-        for k, (t, v0, n) in enumerate(UNITS):
-            first_unit.setdefault(t, k)
-        ended = set()
-        finished = 0
-        for step in range(-WINDOW_LEAD, len(UNITS) + max(LEAD)):
-            for t in range(PACK):
-                if first_unit[t] - WINDOW_LEAD == step:
-                    windows(t)
-                    if t == 0:
-                        quantize_w2()
-            for s in range(6):
-                k = step - LEAD[s]
-                if 0 <= k < len(UNITS):
-                    stage(s, k)
-                    if s == 5:
-                        ended.add(k)
-                        while finished < len(CHUNKS):
-                            c0, cn = CHUNKS[finished]
-                            if not all(i in ended for i, (t, a, b) in enumerate(UNITS) if a < c0 + cn and a + b > c0):
-                                break
-                            finish(c0, cn)
-                            finished = finished + 1
+        stages = ((gather_sums, 0), (rotate, 0), (magnitudes, 1), (larger, 1), (reciprocal, 2), (first_term, 3))
+        last_lag = stages[-1][1]
+        for step in range(-WINDOW_LEAD, len(TASKS) + last_lag):
+            tile_due = step + WINDOW_LEAD
+            if tile_due < PACK:
+                windows(tile_due)
+            if tile_due == 0:
+                round_w2()
+            if tile_due == PACK - 1:
+                quantize_w2()
+            for stage, lag in stages:
+                if 0 <= step - lag < len(TASKS):
+                    stage(step - lag)
+            ended = step - last_lag
+            if ended >= PACK - 1:
+                finish(*TASKS[ended][1:])

@@ -101,7 +101,7 @@ def tile_picked_yrotqv_norm_p_kernel(tc, x_words, x_scales, w1, sg, unit, w2, of
             scale = gain[:, t : t + 1]
             banks = []
             for b in range(2):
-                y = ypsum.tile([P, BANK], F32, name="y")
+                y = ypsum.tile([P, BANK], F32, name="y", tag="y")
                 nc.tensor.matmul_mx(
                     out=y[:],
                     lhsT=w1_codes[:, t * P : (t + 1) * P].bitcast(FP8X4),
@@ -197,10 +197,10 @@ def tile_picked_yrotqv_norm_p_kernel(tc, x_words, x_scales, w1, sg, unit, w2, of
             codes = keep.tile([P, n], U32, name=f"hid_codes{v0}", align_bytes=MX_ALIGN)
             scales = keep.tile([P, n], U8, name=f"hid_scales{v0}", align_bytes=MX_ALIGN)
             nc.vector.quantize_mx(out=codes[:].bitcast(FP8X4), scales=scales[:], in_=grouped[:].rearrange("p c t -> p (c t)"))
-            acc = opsum.tile([P, N // P, n], F32, name="acc")
-            for a in range(N // P):
+
+            def product(a, acc):
                 nc.tensor.matmul_mx(
-                    out=acc[:, a, :],
+                    out=acc,
                     lhsT=held["w2_codes"][:, a * P : (a + 1) * P].bitcast(FP8X4),
                     lhsT_scale=w2_scales[:, a * P : (a + 1) * P],
                     rhs=codes[:].bitcast(FP8X4),
@@ -208,9 +208,21 @@ def tile_picked_yrotqv_norm_p_kernel(tc, x_words, x_scales, w1, sg, unit, w2, of
                     start=True,
                     stop=True,
                 )
-            result = keep.tile([P, N // P, n], F32, name=f"result{v0}")
-            nc.scalar.copy(result[:], acc[:])
-            nc.sync.dma_start(out_rows[:, :, v0 : v0 + n], result[:])
+
+            if v0 + n < V:
+                acc = opsum.tile([P, N // P, n], F32, name="acc")
+                for a in range(N // P):
+                    product(a, acc[:, a, :])
+                result = keep.tile([P, N // P, n], F32, name=f"result{v0}")
+                nc.scalar.copy(result[:], acc[:])
+                nc.sync.dma_start(out_rows[:, :, v0 : v0 + n], result[:])
+            else:
+                for a, copy, store in ((0, nc.vector.tensor_copy, nc.sync.dma_start), (1, nc.scalar.copy, nc.scalar.dma_start)):
+                    acc = ypsum.tile([P, n], F32, name="last_acc", tag="y")
+                    product(a, acc[:])
+                    result = keep.tile([P, n], F32, name=f"last_result{a}")
+                    copy(result[:], acc[:])
+                    store(out_rows[:, a, v0 : v0 + n], result[:])
 
         stages = ((gather_sums, 0), (rotate, 0), (magnitudes, 1), (larger, 1), (reciprocal, 2), (first_term, 3))
         last_lag = stages[-1][1]

from contextlib import ExitStack

import concourse.mybir as mybir

K, T, S, H, V, N = 512, 4096, 1024, 512, 512, 256
FLOPS = 2 * K * H * S + 2 * H * N * V

F32 = mybir.dt.float32
BF16 = mybir.dt.bfloat16
I32 = mybir.dt.int32
U32 = mybir.dt.uint32
U16 = mybir.dt.uint16
U8 = mybir.dt.uint8
FP8X4 = mybir.dt.float8_e4m3fn_x4
ALU = mybir.AluOpType
ACT = mybir.ActivationFunctionType

P = 128
PACK = 4
BANK = 512
PAIRS = BANK // 2
LIST_ROWS = 16
MX_ALIGN = 64
TINY = 2.0**-100

PIECES = ((0, 256), (256, 128), (384, 128))
TASKS = tuple((t, 0, V) for t in range(PACK - 1)) + tuple((PACK - 1, v0, n) for v0, n in PIECES)
WINDOW_LEAD = 2


def tile_picked_yrotqv_norm_p_kernel(tc, x_words, x_scales, w1, sg, unit, w2, offs, ra, rb, out):
    nc = tc.nc
    with ExitStack() as ctx:
        keep = ctx.enter_context(tc.tile_pool(name="keep", bufs=1))
        ypsum = ctx.enter_context(tc.psum_pool(name="ypsum", bufs=6))
        opsum = ctx.enter_context(tc.psum_pool(name="opsum", bufs=2))

        offs_t = keep.tile([P, S // LIST_ROWS], U16, name="offs_t")
        ra_t = keep.tile([P, V // LIST_ROWS], U16, name="ra_t")
        rb_t = keep.tile([P, V // LIST_ROWS], U16, name="rb_t")
        unit_t = keep.tile([P, PACK], F32, name="unit_t", tag="unit_then_words", align_bytes=MX_ALIGN)
        table_scales = keep.tile([P, T], U8, name="table_scales", tag="scales_then_inputs", align_bytes=MX_ALIGN)
        w1_raw = keep.tile([P, PACK, H], F32, name="w1_raw")

        nc.scalar.dma_start(unit_t[:], unit.rearrange("(p t) o -> p (t o)", t=PACK))
        nc.sync.dma_start(offs_t[:], offs)
        nc.sync.dma_start(w1_raw[:], w1.rearrange("(p j) c -> p j c", j=PACK))
        nc.sync.dma_start(ra_t[:], ra)
        nc.sync.dma_start(rb_t[:], rb)
        nc.vector.memset(table_scales[:].bitcast(I32), 0)
        for q in range(4):
            nc.scalar.dma_start(table_scales[32 * q : 32 * q + 4, :].bitcast(I32), x_scales[0, 4 * q : 4 * q + 4, :].bitcast(I32))

        gain = keep.tile([P, PACK], F32, name="gain")
        nc.vector.tensor_scalar(gain[:], unit_t[:], 0.4, None, ALU.mult)
        warm_out = keep.tile([P, 1], F32, name="warm_out")
        nc.scalar.activation(warm_out[:], gain[:, 0:1], ACT.Abs_reciprocal_sqrt)

        table_words = keep.tile([P, T], I32, name="table_words", tag="unit_then_words", align_bytes=MX_ALIGN)
        nc.sync.dma_start(table_words[:], x_words[0].rearrange("p n t -> p (n t)").bitcast(I32))

        picked = [offs_t[:, b * (BANK // LIST_ROWS) : (b + 1) * (BANK // LIST_ROWS)] for b in range(2)]
        x_bytes = []
        for b in range(2):
            gathered_bytes = keep.tile([P, BANK], U8, name=f"x_bytes{b}", align_bytes=MX_ALIGN)
            nc.vector.tensor_copy(gathered_bytes[:], table_scales[:].indirect(picked[b]))
            x_bytes.append(gathered_bytes)

        inputs = keep.tile([P, (1 + PACK) * S], F32, name="inputs", tag="scales_then_inputs", align_bytes=MX_ALIGN)
        w2_raw = inputs[:, 0 : PACK * N].rearrange("p (j c) -> p j c", j=PACK)
        sg_t = [inputs[:, (1 + t) * S : (2 + t) * S] for t in range(PACK)]
        sg_rows = sg.rearrange("(p t) s -> p t s", t=PACK)
        nc.sync.dma_start(sg_t[0], sg_rows[:, 0, :])
        nc.sync.dma_start(w2_raw, w2.rearrange("(p j) c -> p j c", j=PACK))
        for t in range(1, PACK):
            nc.sync.dma_start(sg_t[t], sg_rows[:, t, :])

        x_codes = []
        for b in range(2):
            gathered_words = keep.tile([P, BANK], U32, name=f"x_codes{b}", tag=f"x_codes{b}", align_bytes=MX_ALIGN)
            nc.vector.tensor_copy(gathered_words[:], table_words[:].bitcast(U32).indirect(picked[b]))
            x_codes.append(gathered_words)

        w1_grouped = keep.tile([P, PACK, P, PACK], BF16, name="w1_grouped", align_bytes=MX_ALIGN)
        nc.scalar.copy(w1_grouped[:].rearrange("p t m j -> p m t j"), w1_raw[:].rearrange("p j (m t) -> p m t j", t=PACK))
        w1_codes = keep.tile([P, H], U32, name="w1_codes", align_bytes=MX_ALIGN)
        w1_scales = keep.tile([P, H], U8, name="w1_scales", align_bytes=MX_ALIGN)
        nc.vector.quantize_mx(out=w1_codes[:].bitcast(FP8X4), scales=w1_scales[:], in_=w1_grouped[:].rearrange("p t m j -> p (t m j)"))

        gain_size = keep.tile([P, PACK], F32, name="gain_size")
        nc.vector.scalar_tensor_tensor(gain_size[:], gain[:], -1.0, gain[:], ALU.mult, ALU.max)
        unit_size = keep.tile([P, PACK], F32, name="unit_size")
        nc.vector.tensor_scalar(unit_size[:], gain_size[:], 2.5, None, ALU.mult)
        shift = keep.tile([P, PACK], F32, name="shift")
        nc.vector.tensor_scalar(shift[:], gain_size[:], 0.5, TINY, ALU.mult, ALU.max)

        sum_win = [keep.tile([P, V + V], F32, name=f"sum_win{t}") for t in range(PACK)]
        dif_win = [keep.tile([P, V + S], F32, name=f"dif_win{t}") for t in range(PACK)]

        def windows(t):
            scale = gain[:, t : t + 1]
            banks = []
            for b in range(2):
                y = ypsum.tile([P, BANK], F32, name="y", tag="y")
                nc.tensor.matmul_mx(
                    out=y[:],
                    lhsT=w1_codes[:, t * P : (t + 1) * P].bitcast(FP8X4),
                    lhsT_scale=w1_scales[:, t * P : (t + 1) * P],
                    rhs=x_codes[b][:].bitcast(FP8X4),
                    rhs_scale=x_bytes[b][:],
                    start=True,
                    stop=True,
                )
                banks.append(y)
            odd = [sum_win[t][:, V + b * PAIRS : V + (b + 1) * PAIRS] for b in range(2)]
            for b in range(2):
                nc.scalar.activation(odd[b], banks[b][:, 1::2], ACT.Copy, scale=scale)
            for b in range(2):
                nc.vector.scalar_tensor_tensor(sum_win[t][:, b * PAIRS : (b + 1) * PAIRS], banks[b][:, 0::2], scale, odd[b], ALU.mult, ALU.add)
            for b in range(2):
                nc.vector.scalar_tensor_tensor(
                    dif_win[t][:, V + b * BANK : V + (b + 1) * BANK], banks[b][:], scale, sg_t[t][:, b * BANK : (b + 1) * BANK], ALU.mult, ALU.mult
                )
            adder = nc.gpsimd if t < PACK - 1 else nc.vector
            adder.tensor_tensor(dif_win[t][:, 0:V], dif_win[t][:, V::2], dif_win[t][:, V + 1 :: 2], ALU.add)

        rot = keep.tile([P, PACK, 2, V], F32, name="rot")
        first = keep.tile([P, PACK, V], F32, name="first")
        held = {}

        def fresh(name, k, width):
            held[(name, k)] = keep.tile([P, width], F32, name=f"{name}{k}")
            return held[(name, k)]

        def lists(k):
            v0, n = TASKS[k][1:]
            cols = slice(v0 // LIST_ROWS, (v0 + n) // LIST_ROWS)
            return ra_t[:, cols], rb_t[:, cols]

        def gather_sums(k):
            t, n = TASKS[k][0], TASKS[k][2]
            by_ra, by_rb = lists(k)
            nc.scalar.activation(fresh("sum_a", k, n)[:], sum_win[t][:].indirect(by_ra), ACT.Copy)
            nc.scalar.activation(fresh("sum_b", k, n)[:], sum_win[t][:].indirect(by_rb), ACT.Copy)

        def rotate(k):
            t, v0, n = TASKS[k]
            by_ra, by_rb = lists(k)
            nc.vector.tensor_tensor(rot[:, t, 1, v0 : v0 + n], dif_win[t][:].indirect(by_rb), held[("sum_a", k)][:], ALU.add)
            nc.vector.tensor_tensor(rot[:, t, 0, v0 : v0 + n], dif_win[t][:].indirect(by_ra), held[("sum_b", k)][:], ALU.subtract)

        def magnitudes(k):
            t, v0, n = TASKS[k]
            mag = fresh("mag", k, 2 * n)
            if n == V:
                nc.scalar.activation(mag[:], rot[:, t, :, :].rearrange("p r v -> p (r v)"), ACT.Abs)
            else:
                nc.scalar.activation(mag[:, n : 2 * n], rot[:, t, 1, v0 : v0 + n], ACT.Abs)
                nc.scalar.activation(mag[:, 0:n], rot[:, t, 0, v0 : v0 + n], ACT.Abs)

        def larger(k):
            n = TASKS[k][2]
            mag = held[("mag", k)]
            nc.vector.tensor_tensor(fresh("absm", k, n)[:], mag[:, 0:n], mag[:, n : 2 * n], ALU.max)

        def reciprocal(k):
            t, n = TASKS[k][0], TASKS[k][2]
            nc.scalar.activation(fresh("root", k, n)[:], held[("absm", k)][:], ACT.Abs_reciprocal_sqrt, bias=shift[:, t : t + 1])
            nc.scalar.activation(fresh("recip", k, n)[:], held[("root", k)][:], ACT.Square)

        def first_term(k):
            t, v0, n = TASKS[k]
            nc.vector.scalar_tensor_tensor(
                first[:, t, v0 : v0 + n], rot[:, t, 1, v0 : v0 + n], unit_size[:, t : t + 1], held[("recip", k)][:], ALU.mult, ALU.mult
            )

        w2_grouped = keep.tile([P, N, PACK], BF16, name="w2_grouped", align_bytes=MX_ALIGN)
        w2_scales = keep.tile([P, N], U8, name="w2_scales", align_bytes=MX_ALIGN)

        def round_w2():
            nc.gpsimd.tensor_scalar(w2_grouped[:], w2_raw.rearrange("p j c -> p c j"), 1.0, 0.0, ALU.mult, ALU.add)

        def quantize_w2():
            held["w2_codes"] = keep.tile([P, N], U32, name="w2_codes", tag="x_codes1", align_bytes=MX_ALIGN)
            nc.vector.quantize_mx(out=held["w2_codes"][:].bitcast(FP8X4), scales=w2_scales[:], in_=w2_grouped[:].rearrange("p c j -> p (c j)"))

        out_rows = out.rearrange("(a p) v -> p a v", p=P)

        def finish(v0, n):
            grouped = keep.tile([P, n, PACK], BF16, name=f"hid_grouped{v0}", align_bytes=MX_ALIGN)
            nc.vector.tensor_tensor(
                grouped[:].rearrange("p (c i) t -> p c t i", i=2),
                first[:, :, v0 : v0 + n].rearrange("p t (c i) -> p c t i", i=2),
                rot[:, :, 0, v0 : v0 + n].rearrange("p t (c i) -> p c t i", i=2),
                ALU.subtract,
            )
            codes = keep.tile([P, n], U32, name=f"hid_codes{v0}", align_bytes=MX_ALIGN)
            scales = keep.tile([P, n], U8, name=f"hid_scales{v0}", align_bytes=MX_ALIGN)
            nc.vector.quantize_mx(out=codes[:].bitcast(FP8X4), scales=scales[:], in_=grouped[:].rearrange("p c t -> p (c t)"))

            def product(a, acc):
                nc.tensor.matmul_mx(
                    out=acc,
                    lhsT=held["w2_codes"][:, a * P : (a + 1) * P].bitcast(FP8X4),
                    lhsT_scale=w2_scales[:, a * P : (a + 1) * P],
                    rhs=codes[:].bitcast(FP8X4),
                    rhs_scale=scales[:],
                    start=True,
                    stop=True,
                )

            if v0 + n < V:
                acc = opsum.tile([P, N // P, n], F32, name="acc")
                for a in range(N // P):
                    product(a, acc[:, a, :])
                result = keep.tile([P, N // P, n], F32, name=f"result{v0}")
                nc.scalar.copy(result[:], acc[:])
                nc.sync.dma_start(out_rows[:, :, v0 : v0 + n], result[:])
            else:
                for a, copy, store in ((0, nc.vector.tensor_copy, nc.sync.dma_start), (1, nc.scalar.copy, nc.scalar.dma_start)):
                    acc = ypsum.tile([P, n], F32, name="last_acc", tag="y")
                    product(a, acc[:])
                    result = keep.tile([P, n], F32, name=f"last_result{a}")
                    copy(result[:], acc[:])
                    store(out_rows[:, a, v0 : v0 + n], result[:])

        stages = ((gather_sums, 0), (rotate, 0), (magnitudes, 1), (larger, 1), (reciprocal, 2), (first_term, 3))
        last_lag = stages[-1][1]
        for step in range(-WINDOW_LEAD, len(TASKS) + last_lag):
            tile_due = step + WINDOW_LEAD
            if tile_due < PACK:
                windows(tile_due)
            if tile_due == 0:
                round_w2()
            if tile_due == PACK - 1:
                quantize_w2()
            for stage, lag in stages:
                if 0 <= step - lag < len(TASKS):
                    stage(step - lag)
            ended = step - last_lag
            if ended >= PACK - 1:
                finish(*TASKS[ended][1:])
